import numpy as np
import ml_dtypes


def mxq(x, axis, fmt="e4m3"):
    dtype, down = {"e4m3": (ml_dtypes.float8_e4m3fn, 7), "e5m2": (ml_dtypes.float8_e5m2, 14)}[fmt]
    v = np.moveaxis(np.asarray(x, np.float32).astype(ml_dtypes.bfloat16).astype(np.float64), axis, -1)
    blocks = v.reshape(v.shape[:-1] + (-1, 32))
    amax = np.abs(blocks).max(-1, keepdims=True)
    byte = np.maximum(np.where(amax > 0, np.frexp(amax)[1] - 1 + 127, 0) - down, 1)
    scale = np.exp2(byte - 127.0)
    codes = (blocks / scale).astype(np.float32).astype(dtype).astype(np.float64)
    return np.moveaxis((codes * scale).reshape(v.shape), -1, axis)


WIDE = False


def mx_kscale(k):
    if not WIDE:
        return np.ones(k)
    levels = np.array([30, -30])
    if k % 512:
        return np.exp2(np.random.permutation(np.resize(levels, k // 32))).repeat(32)
    a = np.empty((k // 512, 16))
    for p in range(k // 512):
        a[p, :8] = np.random.permutation(np.resize(levels, 8))
        for g in range(8):
            far = levels[np.abs(levels - a[p, g]) >= 10]
            a[p, g + 8] = far[np.random.randint(len(far))]
    return np.exp2(a.ravel()).repeat(32)


def f64(x):
    return np.asarray(x).astype(np.float64)


def striped(idx):
    return np.tile(np.asarray(idx).reshape(-1, 16).T, (8, 1)).astype(np.uint16)


def unstriped(offs):
    return offs[:16].T.reshape(-1).astype(np.int64)


E2M1 = np.array([0.0, 0.5, 1.0, 1.5, 2.0, 3.0, 4.0, 6.0, -0.0, -0.5, -1.0, -1.5, -2.0, -3.0, -4.0, -6.0])


def pack_weight(w, fmt):
    k, n = w.shape
    w = f64(np.asarray(w, np.float32).astype(ml_dtypes.bfloat16)).reshape(k // 32, 32, n)
    amax = np.abs(w).max(1)
    if fmt in ("e4m3", "e5m2"):
        byte = np.frexp(amax)[1] - 1 + 127 - (7 if fmt == "e4m3" else 14)
    else:
        mant, ex = np.frexp(amax / 6.0)
        byte = np.where(mant > 0.5, ex, ex - 1) + 127
    byte = np.clip(np.where(amax > 0, byte, 1), 1, 254)
    scaled = (w * np.exp2(127.0 - byte)[:, None, :]).reshape(k, n).astype(np.float32)
    by_word = np.ascontiguousarray(scaled.reshape(k // 512, 128, 4, n).transpose(0, 1, 3, 2))
    if fmt in ("e4m3", "e5m2"):
        words = by_word.astype(ml_dtypes.float8_e4m3fn if fmt == "e4m3" else ml_dtypes.float8_e5m2).view(np.uint8)
    else:
        c = by_word.astype(ml_dtypes.float4_e2m1fn).view(np.uint8) & 0xF
        words = (c[..., 0::2] | (c[..., 1::2] << 4)).reshape(k // 512, 128, 2 * n)
    return np.ascontiguousarray(words), np.ascontiguousarray(byte.astype(np.uint8).reshape(k // 512, 16, n))


def unpack_weight(words, scales, fmt):
    g, _, n = scales.shape
    words = np.ascontiguousarray(words).reshape(g, 128, n, -1)
    if fmt in ("e4m3", "e5m2"):
        vals = words.view(ml_dtypes.float8_e4m3fn if fmt == "e4m3" else ml_dtypes.float8_e5m2).astype(np.float64)
    else:
        nib = np.empty((g, 128, n, 4), np.uint8)
        nib[..., 0::2] = words & 0xF
        nib[..., 1::2] = words >> 4
        vals = E2M1[nib]
    vals = vals * np.repeat(np.exp2(scales.astype(np.float64) - 127.0), 8, axis=1)[..., None]
    return vals.transpose(0, 1, 3, 2).reshape(g * 512, n)


K, T, J, R, N, S = 512, 1024, 256, 512, 256, 1024


def setup_inputs():
    n = np.random.standard_normal
    idx = np.random.permutation(T)[:J]
    idx2 = np.random.permutation(J)[:J]
    idx3 = np.random.permutation(J)[:J]
    idx4 = np.random.permutation(S)[:N]
    fk = mx_kscale(K)
    fr = mx_kscale(R)
    xtp = pack_weight(n((K, T)) / fk[:, None], "e5m2")
    wp = pack_weight(n((K, R)) * 1 / np.sqrt(K) * fk[:, None] * fr, "e2m1")
    w2p = pack_weight(n((K, R)) * 1 / np.sqrt(K) * fk[:, None] * fr, "e4m3")
    vsp = pack_weight(n((R, S)) * 1 / np.sqrt(R) / fr[:, None], "e2m1")
    return {
        "xt_words": xtp[0],
        "xt_scales": xtp[1],
        "w_words": wp[0],
        "w_scales": wp[1],
        "w2_words": w2p[0],
        "w2_scales": w2p[1],
        "sa": (np.random.uniform(0.5, 1.6, (R, 1))).astype(np.float32),
        "sb": (np.random.uniform(0.5, 1.6, (R, 1))).astype(np.float32),
        "vs_words": vsp[0],
        "vs_scales": vsp[1],
        "offs": striped(idx),
        "offs2": striped(idx2),
        "offs3": striped(idx3),
        "offs4": striped(idx4),
    }


def reference(xt_words, xt_scales, w_words, w_scales, w2_words, w2_scales, sa, sb, vs_words, vs_scales, offs, offs2, offs3, offs4):
    idx = unstriped(offs)
    idx2 = unstriped(offs2)
    idx3 = unstriped(offs3)
    idx4 = unstriped(offs4)
    xtu = unpack_weight(xt_words, xt_scales, "e5m2")
    wu = unpack_weight(w_words, w_scales, "e2m1")
    w2u = unpack_weight(w2_words, w2_scales, "e4m3")
    vsu = unpack_weight(vs_words, vs_scales, "e2m1")
    xtidxg = xtu[:, idx]
    a = wu.T @ xtidxg
    b = w2u.T @ xtidxg
    hid = np.maximum(a - b[:, idx2] * f64(sa), b - a[:, idx3] * f64(sb))
    vsidx4g = vsu[:, idx4]
    hidq = mxq(hid, 0, "e4m3")
    y = vsidx4g.T @ hidq
    return y

@@ -1,0 +1,188 @@
+from contextlib import ExitStack
+
+import concourse.mybir as mybir
+
+K, T, J, R, N, S = 512, 1024, 256, 512, 256, 1024
+FLOPS = 2 * (2 * K * R * J + R * N * J)
+
+F32 = mybir.dt.float32
+BF16 = mybir.dt.bfloat16
+I32 = mybir.dt.int32
+U32 = mybir.dt.uint32
+U16 = mybir.dt.uint16
+U8 = mybir.dt.uint8
+E4M3 = mybir.dt.float8_e4m3fn_x4
+E5M2 = mybir.dt.float8_e5m2_x4
+E2M1 = mybir.dt.float4_e2m1fn_x4
+COPY = mybir.ActivationFunctionType.Copy
+SUB = mybir.AluOpType.subtract
+MAX = mybir.AluOpType.max
+
+P = 128
+PACK = 4
+HALF = J // 2
+
+
+def tile_list_mutualweighed_twow_store_plain_kernel(
+    tc, xt_words, xt_scales, w_words, w_scales, w2_words, w2_scales, sa, sb,
+    vs_words, vs_scales, offs, offs2, offs3, offs4, out,
+):
+    nc = tc.nc
+    with ExitStack() as ctx:
+        pool = ctx.enter_context(tc.tile_pool(name="sbuf", bufs=1))
+        psum = ctx.enter_context(tc.psum_pool(name="psum", bufs=1))
+
+        def sbuf(name, shape, dtype):
+            return pool.tile(shape, dtype, name=name, align_bytes=64)
+
+        def shared(name, shape, dtype, tag):
+            return pool.tile(shape, dtype, name=name, tag=tag, align_bytes=64)
+
+        def load_scale_rows(queue, plane, scales, quadrants=range(4)):
+            for q in quadrants:
+                queue.dma_start(
+                    out=plane[32 * q : 32 * q + 4, :].bitcast(I32),
+                    in_=scales[0, 4 * q : 4 * q + 4, :].bitcast(I32),
+                )
+
+        list_x = sbuf("list_x", [P, J // 16], U16)
+        list_b = sbuf("list_b", [P, J // 16], U16)
+        list_a = sbuf("list_a", [P, J // 16], U16)
+        list_v = sbuf("list_v", [P, N // 16], U16)
+        xt_w = shared("xt_w", [P, T], U32, "xt_w_w2")
+        xt_s = sbuf("xt_s", [P, T], U8)
+        w_w = sbuf("w_w", [P, R], U16)
+        w_stage = sbuf("w_stage", [4, 4, R], U8)
+        w_s = sbuf("w_s", [P, R], U8)
+        w2_w = shared("w2_w", [P, R], U32, "w2_w_a1")
+        w2_s = shared("w2_s", [P, R], U8, "w2_s_a2")
+        vs_w = shared("vs_w", [P, S], U16, "vs_w_d1")
+        vs_s = shared("vs_s", [P, S], U8, "vs_s_hid")
+        sa_t = sbuf("sa_t", [P, PACK], F32)
+        sb_t = sbuf("sb_t", [P, PACK], F32)
+
+        nc.vector.memset(xt_s[:].bitcast(I32), 0)
+        nc.vector.memset(w_s[:].bitcast(I32), 0)
+        nc.gpsimd.memset(w2_s[:].bitcast(I32), 0)
+        nc.gpsimd.memset(vs_s[:].bitcast(I32), 0)
+
+        nc.sync.dma_start(
+            out=w_stage[:].bitcast(I32),
+            in_=w_scales[0].rearrange("(q r) c -> r q c", r=4).bitcast(I32),
+        )
+        nc.sync.dma_start(list_x[:], offs)
+        nc.sync.dma_start(out=xt_w[:].bitcast(I32), in_=xt_words[0].rearrange("p n t -> p (n t)").bitcast(I32))
+        nc.sync.dma_start(out=w_w[:].bitcast(I32), in_=w_words[0].bitcast(I32))
+        load_scale_rows(nc.scalar, xt_s, xt_scales)
+        nc.gpsimd.dma_start(out=sb_t[:], in_=sb.rearrange("(p t) o -> p (t o)", t=PACK))
+        nc.gpsimd.dma_start(out=sa_t[:], in_=sa.rearrange("(p t) o -> p (t o)", t=PACK))
+        nc.sync.dma_start(list_a[:], offs3)
+        nc.sync.dma_start(out=w2_w[:].bitcast(I32), in_=w2_words[0].rearrange("p n t -> p (n t)").bitcast(I32))
+        load_scale_rows(nc.sync, w2_s, w2_scales)
+        nc.sync.dma_start(list_b[:], offs2)
+        nc.sync.dma_start(out=vs_w[:].bitcast(I32), in_=vs_words[0].bitcast(I32))
+        nc.sync.dma_start(list_v[:], offs4)
+        load_scale_rows(nc.sync, vs_s, vs_scales)
+
+        for q in range(4):
+            nc.vector.tensor_copy(
+                out=w_s[32 * q : 32 * q + 4, :].bitcast(I32), in_=w_stage[:, q, :].bitcast(I32)
+            )
+        w_sd = shared("w_sd", [P, PACK, P], U8, "dealt_scales")
+        w_s_dealt = w_s[:].rearrange("p (m t) -> p t m", t=PACK)
+        nc.gpsimd.tensor_copy(out=w_sd[:, 0, :], in_=w_s_dealt[:, 0, :])
+        nc.gpsimd.tensor_copy(out=w_sd[:, 1:PACK, :], in_=w_s_dealt[:, 1:PACK, :])
+
+        xg_s = pool.tile([P, J], U8, name="xg_s", tag="gathered_scales", align_bytes=64)
+        nc.vector.tensor_copy(out=xg_s[:], in_=xt_s[:].indirect(list_x[:]))
+        xg_w = sbuf("xg_w", [P, J], U32)
+        nc.vector.tensor_copy(out=xg_w[:], in_=xt_w[:].indirect(list_x[:]))
+
+        w_wd = [sbuf("w_wd%d" % t, [P, P], U16) for t in range(PACK)]
+        for t in range(PACK):
+            nc.scalar.copy(out=w_wd[t][:], in_=w_w[:].rearrange("p (m t) -> p t m", t=PACK)[:, t, :])
+        w2_wd = shared("w2_wd", [P, PACK, P], U32, "w2_wd_vg")
+        nc.scalar.copy(
+            out=w2_wd[:].rearrange("p t m -> p m t"),
+            in_=w2_w[:].rearrange("p (m t) -> p m t", t=PACK),
+        )
+
+        bank = [psum.tile([P, 2, J], F32, name="bank%d" % t) for t in range(PACK)]
+        a_tags = ["a0", "a1", "a2", "a3"]
+        a_sb = [shared("a_sb%d" % t, [P, J], F32, a_tags[t]) for t in range(PACK)]
+        b_sb = [sbuf("b_sb%d" % t, [P, J], F32) for t in range(PACK)]
+        ga = [sbuf("ga%d" % t, [P, J], F32) for t in range(PACK)]
+        d2 = [sbuf("d2_%d" % h, [P, PACK, HALF], F32) for h in range(2)]
+
+        def first_product(t):
+            nc.tensor.matmul_mx(
+                out=bank[t][:, 0, :], lhsT=w_wd[t][:].bitcast(E2M1), lhsT_scale=w_sd[:, t, :],
+                rhs=xg_w[:].bitcast(E5M2), rhs_scale=xg_s[:], start=True, stop=True,
+            )
+            if t == 0:
+                nc.scalar.copy(out=a_sb[t][:], in_=bank[t][:, 0, :])
+            else:
+                nc.vector.tensor_copy(out=a_sb[t][:], in_=bank[t][:, 0, :])
+            for h in range(2):
+                nc.scalar.activation(
+                    out=ga[t][:, h * HALF : (h + 1) * HALF],
+                    in_=a_sb[t][:].indirect(list_a[:, 8 * h : 8 * h + 8]),
+                    func=COPY, scale=sb_t[:, t : t + 1],
+                )
+
+        def second_product(t):
+            nc.tensor.matmul_mx(
+                out=bank[t][:, 1, :], lhsT=w2_wd[:, t, :].bitcast(E4M3), lhsT_scale=w2_sd[:, t, :],
+                rhs=xg_w[:].bitcast(E5M2), rhs_scale=xg_s[:], start=True, stop=True,
+            )
+            nc.vector.tensor_copy(out=b_sb[t][:], in_=bank[t][:, 1, :])
+
+        for t in range(PACK):
+            first_product(t)
+        w2_sd = sbuf("w2_sd", [P, PACK, P], U8)
+        nc.gpsimd.tensor_copy(out=w2_sd[:], in_=w2_s[:].rearrange("p (m t) -> p t m", t=PACK))
+        for t in range(PACK):
+            second_product(t)
+
+        for h in range(2):
+            cols = slice(h * HALF, (h + 1) * HALF)
+            for t in range(PACK):
+                nc.gpsimd.tensor_tensor(out=d2[h][:, t, :], in0=b_sb[t][:, cols], in1=ga[t][:, cols], op=SUB)
+        vg_w = shared("vg_w", [P, N], U16, "w2_wd_vg")
+        nc.vector.tensor_copy(out=vg_w[:], in_=vs_w[:].indirect(list_v[:]))
+        vg_s = pool.tile([P, N], U8, name="vg_s", tag="gathered_scales", align_bytes=64)
+        nc.vector.tensor_copy(out=vg_s[:], in_=vs_s[:].indirect(list_v[:]))
+
+        for h in range(2):
+            cols = slice(h * HALF, (h + 1) * HALF)
+            d1 = shared("d1_%d" % h, [P, PACK, HALF], F32, ["vs_w_d1", "vs_s_hid"][h])
+            for t in range(PACK):
+                gb = sbuf("gb%d_%d" % (h, t), [P, HALF], F32)
+                nc.scalar.activation(
+                    out=gb[:], in_=b_sb[t][:].indirect(list_b[:, 8 * h : 8 * h + 8]),
+                    func=COPY, scale=sa_t[:, t : t + 1],
+                )
+                nc.vector.tensor_tensor(out=d1[:, t, :], in0=bank[t][:, 0, cols], in1=gb[:], op=SUB)
+            hid = shared("hid%d" % h, [P, HALF * PACK], BF16, ["vs_s_hid", "hid1"][h])
+            nc.vector.tensor_tensor(
+                out=hid[:].rearrange("p (c i t) -> p c t i", i=4, t=PACK),
+                in0=d1[:].rearrange("p t (c i) -> p c t i", i=4),
+                in1=d2[h][:].rearrange("p t (c i) -> p c t i", i=4),
+                op=MAX,
+            )
+            hid_w = sbuf("hid_w%d" % h, [P, HALF], U32)
+            hid_s = sbuf("hid_s%d" % h, [P, HALF], U8)
+            nc.vector.quantize_mx(out=hid_w[:].bitcast(E4M3), scales=hid_s[:], in_=hid[:])
+            y_sb = sbuf("y_sb%d" % h, [P, 2, HALF], F32)
+            for c in range(2):
+                y_ps = psum.tile([P, HALF], F32, name="y_ps%d_%d" % (h, c))
+                nc.tensor.matmul_mx(
+                    out=y_ps[:], lhsT=vg_w[:, c * P : (c + 1) * P].bitcast(E2M1),
+                    lhsT_scale=vg_s[:, c * P : (c + 1) * P],
+                    rhs=hid_w[:].bitcast(E4M3), rhs_scale=hid_s[:], start=True, stop=True,
+                )
+                if h == 1 and c == 1:
+                    nc.vector.tensor_copy(out=y_sb[:, c, :], in_=y_ps[:])
+                else:
+                    nc.scalar.copy(out=y_sb[:, c, :], in_=y_ps[:])
+            nc.sync.dma_start(out=out.rearrange("(c p) j -> p c j", p=P)[:, :, cols], in_=y_sb[:])

@@ -49,22 +49,25 @@ def tile_list_mutualweighed_twow_store_plain_kernel(
         list_b = sbuf("list_b", [P, J // 16], U16)
         list_a = sbuf("list_a", [P, J // 16], U16)
         list_v = sbuf("list_v", [P, N // 16], U16)
-        xt_w = shared("xt_w", [P, T], U32, "xt_w_w2")
+        xt_w = shared("xt_w", [P, T], U32, "xt_w_vg")
         xt_s = sbuf("xt_s", [P, T], U8)
         w_w = sbuf("w_w", [P, R], U16)
         w_stage = sbuf("w_stage", [4, 4, R], U8)
-        w_s = sbuf("w_s", [P, R], U8)
-        w2_w = shared("w2_w", [P, R], U32, "w2_w_a1")
-        w2_s = shared("w2_s", [P, R], U8, "w2_s_a2")
-        vs_w = shared("vs_w", [P, S], U16, "vs_w_d1")
+        w_s = shared("w_s", [P, R], U8, "w_s_w2_sd")
+        w2_w = sbuf("w2_w", [P, R], U32)
+        w2_s = sbuf("w2_s", [P, R], U8)
+        vs_w = sbuf("vs_w", [P, S], U16)
         vs_s = shared("vs_s", [P, S], U8, "vs_s_hid")
         sa_t = sbuf("sa_t", [P, PACK], F32)
         sb_t = sbuf("sb_t", [P, PACK], F32)
 
         nc.vector.memset(xt_s[:].bitcast(I32), 0)
-        nc.vector.memset(w_s[:].bitcast(I32), 0)
         nc.gpsimd.memset(w2_s[:].bitcast(I32), 0)
-        nc.gpsimd.memset(vs_s[:].bitcast(I32), 0)
+        nc.vector.memset(w_s[:].bitcast(I32), 0)
+        nc.vector.memset(vs_s[:].bitcast(I32), 0)
+        a_sb = [sbuf("a_sb%d" % t, [P, 2 * J], F32) for t in range(PACK)]
+        for t in range(PACK):
+            nc.vector.memset(a_sb[t][:, J:], 0.0)
 
         nc.sync.dma_start(
             out=w_stage[:].bitcast(I32),
@@ -72,14 +75,14 @@ def tile_list_mutualweighed_twow_store_plain_kernel(
         )
         nc.sync.dma_start(list_x[:], offs)
         nc.sync.dma_start(out=xt_w[:].bitcast(I32), in_=xt_words[0].rearrange("p n t -> p (n t)").bitcast(I32))
-        nc.sync.dma_start(out=w_w[:].bitcast(I32), in_=w_words[0].bitcast(I32))
-        load_scale_rows(nc.scalar, xt_s, xt_scales)
-        nc.gpsimd.dma_start(out=sb_t[:], in_=sb.rearrange("(p t) o -> p (t o)", t=PACK))
-        nc.gpsimd.dma_start(out=sa_t[:], in_=sa.rearrange("(p t) o -> p (t o)", t=PACK))
         nc.sync.dma_start(list_a[:], offs3)
+        load_scale_rows(nc.scalar, xt_s, xt_scales)
+        nc.gpsimd.dma_start(out=w_w[:].bitcast(I32), in_=w_words[0].bitcast(I32))
+        nc.gpsimd.dma_start(out=sb_t[:], in_=sb.rearrange("(p t) o -> p (t o)", t=PACK))
         nc.sync.dma_start(out=w2_w[:].bitcast(I32), in_=w2_words[0].rearrange("p n t -> p (n t)").bitcast(I32))
         load_scale_rows(nc.sync, w2_s, w2_scales)
         nc.sync.dma_start(list_b[:], offs2)
+        nc.sync.dma_start(out=sa_t[:], in_=sa.rearrange("(p t) o -> p (t o)", t=PACK))
         nc.sync.dma_start(out=vs_w[:].bitcast(I32), in_=vs_words[0].bitcast(I32))
         nc.sync.dma_start(list_v[:], offs4)
         load_scale_rows(nc.sync, vs_s, vs_scales)
@@ -88,10 +91,12 @@ def tile_list_mutualweighed_twow_store_plain_kernel(
             nc.vector.tensor_copy(
                 out=w_s[32 * q : 32 * q + 4, :].bitcast(I32), in_=w_stage[:, q, :].bitcast(I32)
             )
-        w_sd = shared("w_sd", [P, PACK, P], U8, "dealt_scales")
+        w_sd = sbuf("w_sd", [P, PACK, P], U8)
         w_s_dealt = w_s[:].rearrange("p (m t) -> p t m", t=PACK)
         nc.gpsimd.tensor_copy(out=w_sd[:, 0, :], in_=w_s_dealt[:, 0, :])
         nc.gpsimd.tensor_copy(out=w_sd[:, 1:PACK, :], in_=w_s_dealt[:, 1:PACK, :])
+        w2_sd = shared("w2_sd", [P, PACK, P], U8, "w_s_w2_sd")
+        nc.gpsimd.tensor_copy(out=w2_sd[:], in_=w2_s[:].rearrange("p (m t) -> p t m", t=PACK))
 
         xg_s = pool.tile([P, J], U8, name="xg_s", tag="gathered_scales", align_bytes=64)
         nc.vector.tensor_copy(out=xg_s[:], in_=xt_s[:].indirect(list_x[:]))
@@ -101,18 +106,16 @@ def tile_list_mutualweighed_twow_store_plain_kernel(
         w_wd = [sbuf("w_wd%d" % t, [P, P], U16) for t in range(PACK)]
         for t in range(PACK):
             nc.scalar.copy(out=w_wd[t][:], in_=w_w[:].rearrange("p (m t) -> p t m", t=PACK)[:, t, :])
-        w2_wd = shared("w2_wd", [P, PACK, P], U32, "w2_wd_vg")
-        nc.scalar.copy(
+        w2_wd = shared("w2_wd", [P, PACK, P], I32, "xt_w_vg")
+        nc.vector.tensor_copy(
             out=w2_wd[:].rearrange("p t m -> p m t"),
-            in_=w2_w[:].rearrange("p (m t) -> p m t", t=PACK),
+            in_=w2_w[:].bitcast(I32).rearrange("p (m t) -> p m t", t=PACK),
         )
 
         bank = [psum.tile([P, 2, J], F32, name="bank%d" % t) for t in range(PACK)]
-        a_tags = ["a0", "a1", "a2", "a3"]
-        a_sb = [shared("a_sb%d" % t, [P, J], F32, a_tags[t]) for t in range(PACK)]
         b_sb = [sbuf("b_sb%d" % t, [P, J], F32) for t in range(PACK)]
         ga = [sbuf("ga%d" % t, [P, J], F32) for t in range(PACK)]
-        d2 = [sbuf("d2_%d" % h, [P, PACK, HALF], F32) for h in range(2)]
+        d2 = sbuf("d2", [P, PACK, J], F32)
 
         def first_product(t):
             nc.tensor.matmul_mx(
@@ -120,15 +123,12 @@ def tile_list_mutualweighed_twow_store_plain_kernel(
                 rhs=xg_w[:].bitcast(E5M2), rhs_scale=xg_s[:], start=True, stop=True,
             )
             if t == 0:
-                nc.scalar.copy(out=a_sb[t][:], in_=bank[t][:, 0, :])
+                nc.scalar.copy(out=a_sb[t][:, 0:J], in_=bank[t][:, 0, :])
             else:
-                nc.vector.tensor_copy(out=a_sb[t][:], in_=bank[t][:, 0, :])
-            for h in range(2):
-                nc.scalar.activation(
-                    out=ga[t][:, h * HALF : (h + 1) * HALF],
-                    in_=a_sb[t][:].indirect(list_a[:, 8 * h : 8 * h + 8]),
-                    func=COPY, scale=sb_t[:, t : t + 1],
-                )
+                nc.vector.tensor_copy(out=a_sb[t][:, 0:J], in_=bank[t][:, 0, :])
+            nc.scalar.activation(
+                out=ga[t][:], in_=a_sb[t][:].indirect(list_a[:]), func=COPY, scale=sb_t[:, t : t + 1]
+            )
 
         def second_product(t):
             nc.tensor.matmul_mx(
@@ -136,38 +136,37 @@ def tile_list_mutualweighed_twow_store_plain_kernel(
                 rhs=xg_w[:].bitcast(E5M2), rhs_scale=xg_s[:], start=True, stop=True,
             )
             nc.vector.tensor_copy(out=b_sb[t][:], in_=bank[t][:, 1, :])
+            if t < PACK - 1:
+                nc.gpsimd.tensor_tensor(out=d2[:, t, :], in0=b_sb[t][:], in1=ga[t][:], op=SUB)
 
         for t in range(PACK):
             first_product(t)
-        w2_sd = sbuf("w2_sd", [P, PACK, P], U8)
-        nc.gpsimd.tensor_copy(out=w2_sd[:], in_=w2_s[:].rearrange("p (m t) -> p t m", t=PACK))
         for t in range(PACK):
             second_product(t)
 
-        for h in range(2):
-            cols = slice(h * HALF, (h + 1) * HALF)
-            for t in range(PACK):
-                nc.gpsimd.tensor_tensor(out=d2[h][:, t, :], in0=b_sb[t][:, cols], in1=ga[t][:, cols], op=SUB)
-        vg_w = shared("vg_w", [P, N], U16, "w2_wd_vg")
+        vg_w = shared("vg_w", [P, N], U16, "xt_w_vg")
         nc.vector.tensor_copy(out=vg_w[:], in_=vs_w[:].indirect(list_v[:]))
         vg_s = pool.tile([P, N], U8, name="vg_s", tag="gathered_scales", align_bytes=64)
         nc.vector.tensor_copy(out=vg_s[:], in_=vs_s[:].indirect(list_v[:]))
 
+        last = PACK - 1
+        nc.vector.tensor_tensor(out=d2[:, last, :], in0=bank[last][:, 1, :], in1=ga[last][:], op=SUB)
+
         for h in range(2):
             cols = slice(h * HALF, (h + 1) * HALF)
-            d1 = shared("d1_%d" % h, [P, PACK, HALF], F32, ["vs_w_d1", "vs_s_hid"][h])
+            d1 = shared("d1_%d" % h, [P, PACK, HALF], F32, "vs_s_hid")
             for t in range(PACK):
-                gb = sbuf("gb%d_%d" % (h, t), [P, HALF], F32)
+                gb = shared("gb%d_%d" % (h, t), [P, HALF], F32, "gb%d" % t)
                 nc.scalar.activation(
                     out=gb[:], in_=b_sb[t][:].indirect(list_b[:, 8 * h : 8 * h + 8]),
                     func=COPY, scale=sa_t[:, t : t + 1],
                 )
                 nc.vector.tensor_tensor(out=d1[:, t, :], in0=bank[t][:, 0, cols], in1=gb[:], op=SUB)
-            hid = shared("hid%d" % h, [P, HALF * PACK], BF16, ["vs_s_hid", "hid1"][h])
+            hid = shared("hid%d" % h, [P, HALF * PACK], BF16, "hid%d" % h)
             nc.vector.tensor_tensor(
                 out=hid[:].rearrange("p (c i t) -> p c t i", i=4, t=PACK),
                 in0=d1[:].rearrange("p t (c i) -> p c t i", i=4),
-                in1=d2[h][:].rearrange("p t (c i) -> p c t i", i=4),
+                in1=d2[:, :, cols].rearrange("p t (c i) -> p c t i", i=4),
                 op=MAX,
             )
             hid_w = sbuf("hid_w%d" % h, [P, HALF], U32)

@@ -21,6 +21,7 @@ MAX = mybir.AluOpType.max
 P = 128
 PACK = 4
 HALF = J // 2
+WHOLE = 2
 
 
 def tile_list_mutualweighed_twow_store_plain_kernel(
@@ -54,7 +55,7 @@ def tile_list_mutualweighed_twow_store_plain_kernel(
         w_w = sbuf("w_w", [P, R], U16)
         w_stage = sbuf("w_stage", [4, 4, R], U8)
         w_s = shared("w_s", [P, R], U8, "w_s_w2_sd")
-        w2_w = sbuf("w2_w", [P, R], U32)
+        w2_w = shared("w2_w", [P, R], U32, "w2_w_vg")
         w2_s = sbuf("w2_s", [P, R], U8)
         vs_w = sbuf("vs_w", [P, S], U16)
         vs_s = shared("vs_s", [P, S], U8, "vs_s_hid")
@@ -65,8 +66,8 @@ def tile_list_mutualweighed_twow_store_plain_kernel(
         nc.gpsimd.memset(w2_s[:].bitcast(I32), 0)
         nc.vector.memset(w_s[:].bitcast(I32), 0)
         nc.vector.memset(vs_s[:].bitcast(I32), 0)
-        a_sb = [sbuf("a_sb%d" % t, [P, 2 * J], F32) for t in range(PACK)]
-        for t in range(PACK):
+        a_sb = [sbuf("a_sb%d" % t, [P, 2 * J if t < WHOLE else J], F32) for t in range(PACK)]
+        for t in range(WHOLE):
             nc.vector.memset(a_sb[t][:, J:], 0.0)
 
         nc.sync.dma_start(
@@ -75,16 +76,16 @@ def tile_list_mutualweighed_twow_store_plain_kernel(
         )
         nc.sync.dma_start(list_x[:], offs)
         nc.sync.dma_start(out=xt_w[:].bitcast(I32), in_=xt_words[0].rearrange("p n t -> p (n t)").bitcast(I32))
-        nc.sync.dma_start(list_a[:], offs3)
+        nc.sync.dma_start(list_v[:], offs4)
         load_scale_rows(nc.scalar, xt_s, xt_scales)
         nc.gpsimd.dma_start(out=w_w[:].bitcast(I32), in_=w_words[0].bitcast(I32))
         nc.gpsimd.dma_start(out=sb_t[:], in_=sb.rearrange("(p t) o -> p (t o)", t=PACK))
         nc.sync.dma_start(out=w2_w[:].bitcast(I32), in_=w2_words[0].rearrange("p n t -> p (n t)").bitcast(I32))
+        nc.sync.dma_start(out=vs_w[:].bitcast(I32), in_=vs_words[0].bitcast(I32))
+        nc.sync.dma_start(list_a[:], offs3)
         load_scale_rows(nc.sync, w2_s, w2_scales)
         nc.sync.dma_start(list_b[:], offs2)
         nc.sync.dma_start(out=sa_t[:], in_=sa.rearrange("(p t) o -> p (t o)", t=PACK))
-        nc.sync.dma_start(out=vs_w[:].bitcast(I32), in_=vs_words[0].bitcast(I32))
-        nc.sync.dma_start(list_v[:], offs4)
         load_scale_rows(nc.sync, vs_s, vs_scales)
 
         for q in range(4):
@@ -96,12 +97,17 @@ def tile_list_mutualweighed_twow_store_plain_kernel(
         nc.gpsimd.tensor_copy(out=w_sd[:, 0, :], in_=w_s_dealt[:, 0, :])
         nc.gpsimd.tensor_copy(out=w_sd[:, 1:PACK, :], in_=w_s_dealt[:, 1:PACK, :])
         w2_sd = shared("w2_sd", [P, PACK, P], U8, "w_s_w2_sd")
-        nc.gpsimd.tensor_copy(out=w2_sd[:], in_=w2_s[:].rearrange("p (m t) -> p t m", t=PACK))
+        w2_s_dealt = w2_s[:].rearrange("p (m t) -> p t m", t=PACK)
+        nc.gpsimd.tensor_copy(out=w2_sd[:, 0, :], in_=w2_s_dealt[:, 0, :])
+        nc.gpsimd.tensor_copy(out=w2_sd[:, 1:PACK, :], in_=w2_s_dealt[:, 1:PACK, :])
 
-        xg_s = pool.tile([P, J], U8, name="xg_s", tag="gathered_scales", align_bytes=64)
+        xg_s = shared("xg_s", [P, J], U8, "gathered_scales")
         nc.vector.tensor_copy(out=xg_s[:], in_=xt_s[:].indirect(list_x[:]))
         xg_w = sbuf("xg_w", [P, J], U32)
-        nc.vector.tensor_copy(out=xg_w[:], in_=xt_w[:].indirect(list_x[:]))
+        halves = [slice(h * HALF, (h + 1) * HALF) for h in range(2)]
+        list_halves = [slice(h * HALF // 16, (h + 1) * HALF // 16) for h in range(2)]
+        for h in range(2):
+            nc.vector.tensor_copy(out=xg_w[:, halves[h]], in_=xt_w[:].indirect(list_x[:, list_halves[h]]))
 
         w_wd = [sbuf("w_wd%d" % t, [P, P], U16) for t in range(PACK)]
         for t in range(PACK):
@@ -111,58 +117,65 @@ def tile_list_mutualweighed_twow_store_plain_kernel(
             out=w2_wd[:].rearrange("p t m -> p m t"),
             in_=w2_w[:].bitcast(I32).rearrange("p (m t) -> p m t", t=PACK),
         )
+        vg_w = shared("vg_w", [P, N], U16, "w2_w_vg")
+        nc.vector.tensor_copy(out=vg_w[:], in_=vs_w[:].indirect(list_v[:]))
 
         bank = [psum.tile([P, 2, J], F32, name="bank%d" % t) for t in range(PACK)]
+        first_bank = psum.tile([P, HALF], F32, name="first_bank")
+        a_ps = [[bank[t][:, 0, halves[h]] for h in range(2)] for t in range(PACK)]
+        a_ps[0][0] = first_bank[:]
         b_sb = [sbuf("b_sb%d" % t, [P, J], F32) for t in range(PACK)]
-        ga = [sbuf("ga%d" % t, [P, J], F32) for t in range(PACK)]
         d2 = sbuf("d2", [P, PACK, J], F32)
 
-        def first_product(t):
+        def product(out_ap, words, scales, cols):
             nc.tensor.matmul_mx(
-                out=bank[t][:, 0, :], lhsT=w_wd[t][:].bitcast(E2M1), lhsT_scale=w_sd[:, t, :],
-                rhs=xg_w[:].bitcast(E5M2), rhs_scale=xg_s[:], start=True, stop=True,
+                out=out_ap, lhsT=words, lhsT_scale=scales,
+                rhs=xg_w[:, cols].bitcast(E5M2), rhs_scale=xg_s[:, cols], start=True, stop=True,
             )
+
+        def look_up(out_ap, window, offsets, scale):
+            nc.scalar.activation(out=out_ap, in_=window[:].indirect(offsets), func=COPY, scale=scale)
+
+        ga = []
+        for t in range(PACK):
+            words, scales = w_wd[t][:].bitcast(E2M1), w_sd[:, t, :]
             if t == 0:
-                nc.scalar.copy(out=a_sb[t][:, 0:J], in_=bank[t][:, 0, :])
+                for h in range(2):
+                    product(a_ps[t][h], words, scales, halves[h])
+                    nc.scalar.copy(out=a_sb[t][:, halves[h]], in_=a_ps[t][h])
             else:
+                product(bank[t][:, 0, :], words, scales, slice(0, J))
                 nc.vector.tensor_copy(out=a_sb[t][:, 0:J], in_=bank[t][:, 0, :])
-            nc.scalar.activation(
-                out=ga[t][:], in_=a_sb[t][:].indirect(list_a[:]), func=COPY, scale=sb_t[:, t : t + 1]
-            )
-
-        def second_product(t):
-            nc.tensor.matmul_mx(
-                out=bank[t][:, 1, :], lhsT=w2_wd[:, t, :].bitcast(E4M3), lhsT_scale=w2_sd[:, t, :],
-                rhs=xg_w[:].bitcast(E5M2), rhs_scale=xg_s[:], start=True, stop=True,
-            )
+            if t < WHOLE:
+                ga.append(sbuf("ga%d" % t, [P, J], F32))
+                look_up(ga[t][:], a_sb[t], list_a[:], sb_t[:, t : t + 1])
+            else:
+                ga.append(shared("ga%d_0" % t, [P, HALF], F32, "ga%d" % t))
+                look_up(ga[t][:], a_sb[t], list_a[:, list_halves[0]], sb_t[:, t : t + 1])
+        for t in range(PACK):
+            product(bank[t][:, 1, :], w2_wd[:, t, :].bitcast(E4M3), w2_sd[:, t, :], slice(0, J))
             nc.vector.tensor_copy(out=b_sb[t][:], in_=bank[t][:, 1, :])
-            if t < PACK - 1:
+            if t < WHOLE:
                 nc.gpsimd.tensor_tensor(out=d2[:, t, :], in0=b_sb[t][:], in1=ga[t][:], op=SUB)
+        for t in range(WHOLE, PACK):
+            nc.vector.tensor_tensor(out=d2[:, t, halves[0]], in0=bank[t][:, 1, halves[0]], in1=ga[t][:], op=SUB)
 
-        for t in range(PACK):
-            first_product(t)
-        for t in range(PACK):
-            second_product(t)
-
-        vg_w = shared("vg_w", [P, N], U16, "xt_w_vg")
-        nc.vector.tensor_copy(out=vg_w[:], in_=vs_w[:].indirect(list_v[:]))
-        vg_s = pool.tile([P, N], U8, name="vg_s", tag="gathered_scales", align_bytes=64)
+        vg_s = shared("vg_s", [P, N], U8, "gathered_scales")
         nc.vector.tensor_copy(out=vg_s[:], in_=vs_s[:].indirect(list_v[:]))
 
-        last = PACK - 1
-        nc.vector.tensor_tensor(out=d2[:, last, :], in0=bank[last][:, 1, :], in1=ga[last][:], op=SUB)
-
         for h in range(2):
-            cols = slice(h * HALF, (h + 1) * HALF)
+            cols = halves[h]
+            if h == 1:
+                for t in range(WHOLE, PACK):
+                    ga_rest = shared("ga%d_1" % t, [P, HALF], F32, "ga%d" % t)
+                    look_up(ga_rest[:], a_sb[t], list_a[:, list_halves[h]], sb_t[:, t : t + 1])
+                    nc.gpsimd.tensor_tensor(out=d2[:, t, cols], in0=b_sb[t][:, cols], in1=ga_rest[:], op=SUB)
             d1 = shared("d1_%d" % h, [P, PACK, HALF], F32, "vs_s_hid")
             for t in range(PACK):
                 gb = shared("gb%d_%d" % (h, t), [P, HALF], F32, "gb%d" % t)
-                nc.scalar.activation(
-                    out=gb[:], in_=b_sb[t][:].indirect(list_b[:, 8 * h : 8 * h + 8]),
-                    func=COPY, scale=sa_t[:, t : t + 1],
-                )
-                nc.vector.tensor_tensor(out=d1[:, t, :], in0=bank[t][:, 0, cols], in1=gb[:], op=SUB)
-            hid = shared("hid%d" % h, [P, HALF * PACK], BF16, "hid%d" % h)
+                look_up(gb[:], b_sb[t], list_b[:, list_halves[h]], sa_t[:, t : t + 1])
+                nc.vector.tensor_tensor(out=d1[:, t, :], in0=a_ps[t][h], in1=gb[:], op=SUB)
+            hid = sbuf("hid%d" % h, [P, HALF * PACK], BF16)
             nc.vector.tensor_tensor(
                 out=hid[:].rearrange("p (c i t) -> p c t i", i=4, t=PACK),
                 in0=d1[:].rearrange("p t (c i) -> p c t i", i=4),
@@ -172,16 +185,24 @@ def tile_list_mutualweighed_twow_store_plain_kernel(
             hid_w = sbuf("hid_w%d" % h, [P, HALF], U32)
             hid_s = sbuf("hid_s%d" % h, [P, HALF], U8)
             nc.vector.quantize_mx(out=hid_w[:].bitcast(E4M3), scales=hid_s[:], in_=hid[:])
-            y_sb = sbuf("y_sb%d" % h, [P, 2, HALF], F32)
+            if h == 0:
+                y_bank = psum.tile([P, 2, HALF], F32, name="y_bank")
+                y_ps = [y_bank[:, c, :] for c in range(2)]
+            else:
+                y_ps = [psum.tile([P, HALF], F32, name="y_bank%d" % c)[:] for c in range(2)]
             for c in range(2):
-                y_ps = psum.tile([P, HALF], F32, name="y_ps%d_%d" % (h, c))
                 nc.tensor.matmul_mx(
-                    out=y_ps[:], lhsT=vg_w[:, c * P : (c + 1) * P].bitcast(E2M1),
+                    out=y_ps[c], lhsT=vg_w[:, c * P : (c + 1) * P].bitcast(E2M1),
                     lhsT_scale=vg_s[:, c * P : (c + 1) * P],
                     rhs=hid_w[:].bitcast(E4M3), rhs_scale=hid_s[:], start=True, stop=True,
                 )
-                if h == 1 and c == 1:
-                    nc.vector.tensor_copy(out=y_sb[:, c, :], in_=y_ps[:])
-                else:
-                    nc.scalar.copy(out=y_sb[:, c, :], in_=y_ps[:])
-            nc.sync.dma_start(out=out.rearrange("(c p) j -> p c j", p=P)[:, :, cols], in_=y_sb[:])
+            if h == 0:
+                y_sb = sbuf("y_sb", [P, 2, HALF], F32)
+                nc.scalar.copy(out=y_sb[:], in_=y_bank[:])
+                nc.sync.dma_start(out=out.rearrange("(c p) j -> p c j", p=P)[:, :, cols], in_=y_sb[:])
+            else:
+                y_last = [sbuf("y_last%d" % c, [P, HALF], F32) for c in range(2)]
+                nc.scalar.copy(out=y_last[0][:], in_=y_ps[0])
+                nc.scalar.dma_start(out=out[0:P, cols], in_=y_last[0][:])
+                nc.vector.tensor_copy(out=y_last[1][:], in_=y_ps[1])
+                nc.sync.dma_start(out=out[P:N, cols], in_=y_last[1][:])

@@ -55,7 +55,7 @@ def tile_list_mutualweighed_twow_store_plain_kernel(
         w_w = sbuf("w_w", [P, R], U16)
         w_stage = sbuf("w_stage", [4, 4, R], U8)
         w_s = shared("w_s", [P, R], U8, "w_s_w2_sd")
-        w2_w = shared("w2_w", [P, R], U32, "w2_w_vg")
+        w2_w = sbuf("w2_w", [P, R], U32)
         w2_s = sbuf("w2_s", [P, R], U8)
         vs_w = sbuf("vs_w", [P, S], U16)
         vs_s = shared("vs_s", [P, S], U8, "vs_s_hid")
@@ -76,13 +76,13 @@ def tile_list_mutualweighed_twow_store_plain_kernel(
         )
         nc.sync.dma_start(list_x[:], offs)
         nc.sync.dma_start(out=xt_w[:].bitcast(I32), in_=xt_words[0].rearrange("p n t -> p (n t)").bitcast(I32))
-        nc.sync.dma_start(list_v[:], offs4)
+        nc.sync.dma_start(list_a[:], offs3)
         load_scale_rows(nc.scalar, xt_s, xt_scales)
         nc.gpsimd.dma_start(out=w_w[:].bitcast(I32), in_=w_words[0].bitcast(I32))
         nc.gpsimd.dma_start(out=sb_t[:], in_=sb.rearrange("(p t) o -> p (t o)", t=PACK))
         nc.sync.dma_start(out=w2_w[:].bitcast(I32), in_=w2_words[0].rearrange("p n t -> p (n t)").bitcast(I32))
         nc.sync.dma_start(out=vs_w[:].bitcast(I32), in_=vs_words[0].bitcast(I32))
-        nc.sync.dma_start(list_a[:], offs3)
+        nc.sync.dma_start(list_v[:], offs4)
         load_scale_rows(nc.sync, w2_s, w2_scales)
         nc.sync.dma_start(list_b[:], offs2)
         nc.sync.dma_start(out=sa_t[:], in_=sa.rearrange("(p t) o -> p (t o)", t=PACK))
@@ -109,7 +109,7 @@ def tile_list_mutualweighed_twow_store_plain_kernel(
         for h in range(2):
             nc.vector.tensor_copy(out=xg_w[:, halves[h]], in_=xt_w[:].indirect(list_x[:, list_halves[h]]))
 
-        w_wd = [sbuf("w_wd%d" % t, [P, P], U16) for t in range(PACK)]
+        w_wd = [shared("w_wd%d" % t, [P, P], U16, "w_wd%d" % t) for t in range(PACK)]
         for t in range(PACK):
             nc.scalar.copy(out=w_wd[t][:], in_=w_w[:].rearrange("p (m t) -> p t m", t=PACK)[:, t, :])
         w2_wd = shared("w2_wd", [P, PACK, P], I32, "xt_w_vg")
@@ -117,8 +117,6 @@ def tile_list_mutualweighed_twow_store_plain_kernel(
             out=w2_wd[:].rearrange("p t m -> p m t"),
             in_=w2_w[:].bitcast(I32).rearrange("p (m t) -> p m t", t=PACK),
         )
-        vg_w = shared("vg_w", [P, N], U16, "w2_w_vg")
-        nc.vector.tensor_copy(out=vg_w[:], in_=vs_w[:].indirect(list_v[:]))
 
         bank = [psum.tile([P, 2, J], F32, name="bank%d" % t) for t in range(PACK)]
         first_bank = psum.tile([P, HALF], F32, name="first_bank")
@@ -146,6 +144,9 @@ def tile_list_mutualweighed_twow_store_plain_kernel(
             else:
                 product(bank[t][:, 0, :], words, scales, slice(0, J))
                 nc.vector.tensor_copy(out=a_sb[t][:, 0:J], in_=bank[t][:, 0, :])
+            if t == 1:
+                vg_w = shared("vg_w", [P, N], U16, "w_wd1")
+                nc.vector.tensor_copy(out=vg_w[:], in_=vs_w[:].indirect(list_v[:]))
             if t < WHOLE:
                 ga.append(sbuf("ga%d" % t, [P, J], F32))
                 look_up(ga[t][:], a_sb[t], list_a[:], sb_t[:, t : t + 1])
@@ -169,7 +170,7 @@ def tile_list_mutualweighed_twow_store_plain_kernel(
                 for t in range(WHOLE, PACK):
                     ga_rest = shared("ga%d_1" % t, [P, HALF], F32, "ga%d" % t)
                     look_up(ga_rest[:], a_sb[t], list_a[:, list_halves[h]], sb_t[:, t : t + 1])
-                    nc.gpsimd.tensor_tensor(out=d2[:, t, cols], in0=b_sb[t][:, cols], in1=ga_rest[:], op=SUB)
+                    nc.vector.tensor_tensor(out=d2[:, t, cols], in0=bank[t][:, 1, cols], in1=ga_rest[:], op=SUB)
             d1 = shared("d1_%d" % h, [P, PACK, HALF], F32, "vs_s_hid")
             for t in range(PACK):
                 gb = shared("gb%d_%d" % (h, t), [P, HALF], F32, "gb%d" % t)

from contextlib import ExitStack

import concourse.mybir as mybir

K, T, J, R, N, S = 512, 1024, 256, 512, 256, 1024
FLOPS = 2 * (2 * K * R * J + R * N * J)

F32 = mybir.dt.float32
BF16 = mybir.dt.bfloat16
I32 = mybir.dt.int32
U32 = mybir.dt.uint32
U16 = mybir.dt.uint16
U8 = mybir.dt.uint8
E4M3 = mybir.dt.float8_e4m3fn_x4
E5M2 = mybir.dt.float8_e5m2_x4
E2M1 = mybir.dt.float4_e2m1fn_x4
COPY = mybir.ActivationFunctionType.Copy
SUB = mybir.AluOpType.subtract
MAX = mybir.AluOpType.max

P = 128
PACK = 4
HALF = J // 2
WHOLE = 2


def tile_list_mutualweighed_twow_store_plain_kernel(
    tc, xt_words, xt_scales, w_words, w_scales, w2_words, w2_scales, sa, sb,
    vs_words, vs_scales, offs, offs2, offs3, offs4, out,
):
    nc = tc.nc
    with ExitStack() as ctx:
        pool = ctx.enter_context(tc.tile_pool(name="sbuf", bufs=1))
        psum = ctx.enter_context(tc.psum_pool(name="psum", bufs=1))

        def sbuf(name, shape, dtype):
            return pool.tile(shape, dtype, name=name, align_bytes=64)

        def shared(name, shape, dtype, tag):
            return pool.tile(shape, dtype, name=name, tag=tag, align_bytes=64)

        def load_scale_rows(queue, plane, scales, quadrants=range(4)):
            for q in quadrants:
                queue.dma_start(
                    out=plane[32 * q : 32 * q + 4, :].bitcast(I32),
                    in_=scales[0, 4 * q : 4 * q + 4, :].bitcast(I32),
                )

        list_x = sbuf("list_x", [P, J // 16], U16)
        list_b = sbuf("list_b", [P, J // 16], U16)
        list_a = sbuf("list_a", [P, J // 16], U16)
        list_v = sbuf("list_v", [P, N // 16], U16)
        xt_w = shared("xt_w", [P, T], U32, "xt_w_vg")
        xt_s = sbuf("xt_s", [P, T], U8)
        w_w = sbuf("w_w", [P, R], U16)
        w_stage = sbuf("w_stage", [4, 4, R], U8)
        w_s = shared("w_s", [P, R], U8, "w_s_w2_sd")
        w2_w = sbuf("w2_w", [P, R], U32)
        w2_s = sbuf("w2_s", [P, R], U8)
        vs_w = sbuf("vs_w", [P, S], U16)
        vs_s = shared("vs_s", [P, S], U8, "vs_s_hid")
        sa_t = sbuf("sa_t", [P, PACK], F32)
        sb_t = sbuf("sb_t", [P, PACK], F32)

        nc.vector.memset(xt_s[:].bitcast(I32), 0)
        nc.gpsimd.memset(w2_s[:].bitcast(I32), 0)
        nc.vector.memset(w_s[:].bitcast(I32), 0)
        nc.vector.memset(vs_s[:].bitcast(I32), 0)
        a_sb = [sbuf("a_sb%d" % t, [P, 2 * J if t < WHOLE else J], F32) for t in range(PACK)]
        for t in range(WHOLE):
            nc.vector.memset(a_sb[t][:, J:], 0.0)

        nc.sync.dma_start(
            out=w_stage[:].bitcast(I32),
            in_=w_scales[0].rearrange("(q r) c -> r q c", r=4).bitcast(I32),
        )
        nc.sync.dma_start(list_x[:], offs)
        nc.sync.dma_start(out=xt_w[:].bitcast(I32), in_=xt_words[0].rearrange("p n t -> p (n t)").bitcast(I32))
        nc.sync.dma_start(list_a[:], offs3)
        load_scale_rows(nc.scalar, xt_s, xt_scales)
        nc.gpsimd.dma_start(out=w_w[:].bitcast(I32), in_=w_words[0].bitcast(I32))
        nc.gpsimd.dma_start(out=sb_t[:], in_=sb.rearrange("(p t) o -> p (t o)", t=PACK))
        nc.sync.dma_start(out=w2_w[:].bitcast(I32), in_=w2_words[0].rearrange("p n t -> p (n t)").bitcast(I32))
        nc.sync.dma_start(out=vs_w[:].bitcast(I32), in_=vs_words[0].bitcast(I32))
        nc.sync.dma_start(list_v[:], offs4)
        load_scale_rows(nc.sync, w2_s, w2_scales)
        nc.sync.dma_start(list_b[:], offs2)
        nc.sync.dma_start(out=sa_t[:], in_=sa.rearrange("(p t) o -> p (t o)", t=PACK))
        load_scale_rows(nc.sync, vs_s, vs_scales)

        for q in range(4):
            nc.vector.tensor_copy(
                out=w_s[32 * q : 32 * q + 4, :].bitcast(I32), in_=w_stage[:, q, :].bitcast(I32)
            )
        w_sd = sbuf("w_sd", [P, PACK, P], U8)
        w_s_dealt = w_s[:].rearrange("p (m t) -> p t m", t=PACK)
        nc.gpsimd.tensor_copy(out=w_sd[:, 0, :], in_=w_s_dealt[:, 0, :])
        nc.gpsimd.tensor_copy(out=w_sd[:, 1:PACK, :], in_=w_s_dealt[:, 1:PACK, :])
        w2_sd = shared("w2_sd", [P, PACK, P], U8, "w_s_w2_sd")
        w2_s_dealt = w2_s[:].rearrange("p (m t) -> p t m", t=PACK)
        nc.gpsimd.tensor_copy(out=w2_sd[:, 0, :], in_=w2_s_dealt[:, 0, :])
        nc.gpsimd.tensor_copy(out=w2_sd[:, 1:PACK, :], in_=w2_s_dealt[:, 1:PACK, :])

        xg_s = shared("xg_s", [P, J], U8, "gathered_scales")
        nc.vector.tensor_copy(out=xg_s[:], in_=xt_s[:].indirect(list_x[:]))
        xg_w = sbuf("xg_w", [P, J], U32)
        halves = [slice(h * HALF, (h + 1) * HALF) for h in range(2)]
        list_halves = [slice(h * HALF // 16, (h + 1) * HALF // 16) for h in range(2)]
        for h in range(2):
            nc.vector.tensor_copy(out=xg_w[:, halves[h]], in_=xt_w[:].indirect(list_x[:, list_halves[h]]))

        w_wd = [shared("w_wd%d" % t, [P, P], U16, "w_wd%d" % t) for t in range(PACK)]
        for t in range(PACK):
            nc.scalar.copy(out=w_wd[t][:], in_=w_w[:].rearrange("p (m t) -> p t m", t=PACK)[:, t, :])
        w2_wd = shared("w2_wd", [P, PACK, P], I32, "xt_w_vg")
        nc.vector.tensor_copy(
            out=w2_wd[:].rearrange("p t m -> p m t"),
            in_=w2_w[:].bitcast(I32).rearrange("p (m t) -> p m t", t=PACK),
        )

        bank = [psum.tile([P, 2, J], F32, name="bank%d" % t) for t in range(PACK)]
        first_bank = psum.tile([P, HALF], F32, name="first_bank")
        a_ps = [[bank[t][:, 0, halves[h]] for h in range(2)] for t in range(PACK)]
        a_ps[0][0] = first_bank[:]
        b_sb = [sbuf("b_sb%d" % t, [P, J], F32) for t in range(PACK)]
        d2 = sbuf("d2", [P, PACK, J], F32)

        def product(out_ap, words, scales, cols):
            nc.tensor.matmul_mx(
                out=out_ap, lhsT=words, lhsT_scale=scales,
                rhs=xg_w[:, cols].bitcast(E5M2), rhs_scale=xg_s[:, cols], start=True, stop=True,
            )

        def look_up(out_ap, window, offsets, scale):
            nc.scalar.activation(out=out_ap, in_=window[:].indirect(offsets), func=COPY, scale=scale)

        ga = []
        for t in range(PACK):
            words, scales = w_wd[t][:].bitcast(E2M1), w_sd[:, t, :]
            if t == 0:
                for h in range(2):
                    product(a_ps[t][h], words, scales, halves[h])
                    nc.scalar.copy(out=a_sb[t][:, halves[h]], in_=a_ps[t][h])
            else:
                product(bank[t][:, 0, :], words, scales, slice(0, J))
                nc.vector.tensor_copy(out=a_sb[t][:, 0:J], in_=bank[t][:, 0, :])
            if t == 1:
                vg_w = shared("vg_w", [P, N], U16, "w_wd1")
                nc.vector.tensor_copy(out=vg_w[:], in_=vs_w[:].indirect(list_v[:]))
            if t < WHOLE:
                ga.append(sbuf("ga%d" % t, [P, J], F32))
                look_up(ga[t][:], a_sb[t], list_a[:], sb_t[:, t : t + 1])
            else:
                ga.append(shared("ga%d_0" % t, [P, HALF], F32, "ga%d" % t))
                look_up(ga[t][:], a_sb[t], list_a[:, list_halves[0]], sb_t[:, t : t + 1])
        for t in range(PACK):
            product(bank[t][:, 1, :], w2_wd[:, t, :].bitcast(E4M3), w2_sd[:, t, :], slice(0, J))
            nc.vector.tensor_copy(out=b_sb[t][:], in_=bank[t][:, 1, :])
            if t < WHOLE:
                nc.gpsimd.tensor_tensor(out=d2[:, t, :], in0=b_sb[t][:], in1=ga[t][:], op=SUB)
        for t in range(WHOLE, PACK):
            nc.vector.tensor_tensor(out=d2[:, t, halves[0]], in0=bank[t][:, 1, halves[0]], in1=ga[t][:], op=SUB)

        vg_s = shared("vg_s", [P, N], U8, "gathered_scales")
        nc.vector.tensor_copy(out=vg_s[:], in_=vs_s[:].indirect(list_v[:]))

        for h in range(2):
            cols = halves[h]
            if h == 1:
                for t in range(WHOLE, PACK):
                    ga_rest = shared("ga%d_1" % t, [P, HALF], F32, "ga%d" % t)
                    look_up(ga_rest[:], a_sb[t], list_a[:, list_halves[h]], sb_t[:, t : t + 1])
                    nc.vector.tensor_tensor(out=d2[:, t, cols], in0=bank[t][:, 1, cols], in1=ga_rest[:], op=SUB)
            d1 = shared("d1_%d" % h, [P, PACK, HALF], F32, "vs_s_hid")
            for t in range(PACK):
                gb = shared("gb%d_%d" % (h, t), [P, HALF], F32, "gb%d" % t)
                look_up(gb[:], b_sb[t], list_b[:, list_halves[h]], sa_t[:, t : t + 1])
                nc.vector.tensor_tensor(out=d1[:, t, :], in0=a_ps[t][h], in1=gb[:], op=SUB)
            hid = sbuf("hid%d" % h, [P, HALF * PACK], BF16)
            nc.vector.tensor_tensor(
                out=hid[:].rearrange("p (c i t) -> p c t i", i=4, t=PACK),
                in0=d1[:].rearrange("p t (c i) -> p c t i", i=4),
                in1=d2[:, :, cols].rearrange("p t (c i) -> p c t i", i=4),
                op=MAX,
            )
            hid_w = sbuf("hid_w%d" % h, [P, HALF], U32)
            hid_s = sbuf("hid_s%d" % h, [P, HALF], U8)
            nc.vector.quantize_mx(out=hid_w[:].bitcast(E4M3), scales=hid_s[:], in_=hid[:])
            if h == 0:
                y_bank = psum.tile([P, 2, HALF], F32, name="y_bank")
                y_ps = [y_bank[:, c, :] for c in range(2)]
            else:
                y_ps = [psum.tile([P, HALF], F32, name="y_bank%d" % c)[:] for c in range(2)]
            for c in range(2):
                nc.tensor.matmul_mx(
                    out=y_ps[c], lhsT=vg_w[:, c * P : (c + 1) * P].bitcast(E2M1),
                    lhsT_scale=vg_s[:, c * P : (c + 1) * P],
                    rhs=hid_w[:].bitcast(E4M3), rhs_scale=hid_s[:], start=True, stop=True,
                )
            if h == 0:
                y_sb = sbuf("y_sb", [P, 2, HALF], F32)
                nc.scalar.copy(out=y_sb[:], in_=y_bank[:])
                nc.sync.dma_start(out=out.rearrange("(c p) j -> p c j", p=P)[:, :, cols], in_=y_sb[:])
            else:
                y_last = [sbuf("y_last%d" % c, [P, HALF], F32) for c in range(2)]
                nc.scalar.copy(out=y_last[0][:], in_=y_ps[0])
                nc.scalar.dma_start(out=out[0:P, cols], in_=y_last[0][:])
                nc.vector.tensor_copy(out=y_last[1][:], in_=y_ps[1])
                nc.sync.dma_start(out=out[P:N, cols], in_=y_last[1][:])
